import numpy as np, ml_dtypes
CORES = [30,158,46,174,86,214]
N = 6
QP = 128
WID = [128,128,16,96,96,64]
def setup_inputs(rng):
    return {"q": rng.standard_normal((N, 128, QP), dtype=np.float32).astype(ml_dtypes.bfloat16), "k": rng.standard_normal((N, 128, 128), dtype=np.float32).astype(ml_dtypes.bfloat16), "v": rng.standard_normal((N, 128, 128), dtype=np.float32).astype(ml_dtypes.bfloat16)}
def setup_inputs_big(rng):
    d = setup_inputs(rng)
    for k in ("q", "k", "v"): d[k] = (d[k].astype(np.float32) * 1024.0).astype(d[k].dtype)
    return d
def setup_inputs_small(rng):
    d = setup_inputs(rng)
    for k in ("q", "k", "v"): d[k] = (d[k].astype(np.float32) * (1 / 1024.0)).astype(d[k].dtype)
    return d
def setup_inputs_apart(rng):
    d = setup_inputs(rng)
    f = (10.0 ** rng.permutation(np.linspace(-1.5, 1.5, N))).astype(np.float32).reshape(N, 1, 1)
    for k in ("q", "k", "v"): d[k] = (d[k].astype(np.float32) * f).astype(d[k].dtype)
    return d
def whole(q, k, v):
    Q, K, V = q.astype(np.float64), k.astype(np.float64), v.astype(np.float64)
    y = np.zeros((N, 128, QP))
    for r in range(N):
        S = [K[j].T @ Q[r] for j in range(N)]
        m = np.max([s.max(axis=0) for s in S], axis=0)
        y[r] = sum(V[j].T @ np.maximum(S[j] - 0.5 * m, 0.0) for j in range(N))
    return {"y": y.astype(ml_dtypes.bfloat16)}
def reference(q, k, v):
    o = whole(q, k, v)["y"].copy()
    for r in range(N):
        o[r][:, WID[r]:] = np.nan
    return {"y": o}

@@ -1,0 +1,150 @@
+from concourse.bass import DstId, RemoteDMATransfer
+from concourse.mybir import dt, AluOpType
+
+NR = 6
+BF = "bfloat16"
+SCRATCH = {
+    "kv": ("sbuf", [128, NR * 256], BF),
+    "qs": ("sbuf", [128, 128], BF),
+    "zsrc": ("sbuf", [128, 129], BF),
+    "idd": ("dram", [129, 128], BF),
+    "ident": ("sbuf", [128, 128], BF),
+    "zero": ("sbuf", [128, 128], BF),
+    "nh": ("sbuf", [128, 128], BF),
+    "mrow": ("sbuf", [128, 128], BF),
+    "run": ("sbuf", [128, 2 * NR * 64], BF),
+    "tr": ("sbuf", [128, 64], BF),
+    "P": ("sbuf", [128, NR * 128], BF),
+    "yo": ("sbuf", [128, 128], BF),
+}
+for _b in range(8):
+    SCRATCH["ps%d" % _b] = ("psum", [128, 512], "float32")
+SEMAPHORES = (["ldk", "ldv", "ldq", "id1", "id2", "sent", "vc", "tm", "ym", "sty"]
+              + ["a%d" % j for j in range(NR)] + ["st%d" % j for j in range(NR)] + ["bm%d" % j for j in range(NR)])
+
+
+def rank_program(g, core, T, topo):
+    r = T.rank_of(core)
+    if r is None:
+        return
+    n = len(T.cores)
+    w = T.tables["WID"][r]
+    sem = T.sem
+    MAX = AluOpType.max
+    send_to = [(r + t) % n for t in range(1, n)]
+    order = [r] + [(r - t) % n for t in range(1, n)]
+
+    def slot(j):
+        return T.kv[:, j * 256:(j + 1) * 256]
+
+    def kk(j):
+        return T.kv[:, j * 256:j * 256 + 128]
+
+    def vv(j):
+        return T.kv[:, j * 256 + 128:(j + 1) * 256]
+
+    g.sync.dma_start(kk(r), T.k[:, :]).then_inc(sem.ldk, 16)
+    g.scalar.dma_start(vv(r), T.v[:, :]).then_inc(sem.ldv, 16)
+    g.sync.dma_start(T.qs[:, 0:w], T.q[:, 0:w]).then_inc(sem.ldq, 16)
+
+    mask = topo.mask(core, T.cores[send_to[0]])
+    for j in send_to:
+        mask &= topo.mask(core, T.cores[j])
+    ne = bin(mask).count("1")
+    ids = []
+    for j in send_to:
+        rid, pid = topo.addr(T.cores[j], core)
+        ids.append(DstId(rid=rid, pnc=pid))
+    g.wait_ge(sem.ldk, 16)
+    g.wait_ge(sem.ldv, 16)
+    g.remote_dma_fused([RemoteDMATransfer(dst_ids=ids, dma_engine_mask=mask, remote_sem=sem["a%d" % r],
+                                          srcs=[slot(r)], dsts=[slot(r) for _ in send_to], alu_op=0)],
+                       local_sem=sem.sent)
+
+    vc = [0]
+
+    def vop(ins):
+        ins.then_inc(sem.vc, 1)
+        vc[0] += 1
+        return vc[0]
+
+    def vwait():
+        if vc[0]:
+            g.vector.wait_ge(sem.vc, vc[0])
+
+    vop(g.vector.memset(T.zsrc[:, 1:129], 0.0))
+    vwait()
+    n_pat = vop(g.vector.memset(T.zsrc[:, 0:1], 1.0))
+    vwait()
+    vop(g.vector.memset(T.zero[:, 0:w], 0.0))
+    vwait()
+    vop(g.vector.memset(T.nh[0:1, :], -0.5))
+
+    g.scalar.wait_ge(sem.vc, n_pat)
+    g.scalar.dma_start(T.idd[:, :], T.zsrc[:, :]).then_inc(sem.id1, 16)
+    g.scalar.wait_ge(sem.id1, 16)
+    g.scalar.dma_start(T.ident[:, :], T.idd[0:128, :]).then_inc(sem.id2, 16)
+
+    bankS = [T["ps%d" % i] for i in range(n)]
+    bankT = [T.ps6, T.ps7]
+
+    g.tensor.wait_ge(sem.ldq, 16)
+    seen = []
+    nrun = 0
+    for i, j in enumerate(order):
+        if i == 0:
+            g.tensor.wait_ge(sem.ldk, 16)
+        else:
+            g.tensor.wait_ge(sem["a%d" % j], ne)
+        if i >= 2:
+            g.tensor.wait_ge(sem.vc, seen[i - 2])
+        st = bankT[i % 2]
+        g.tensor.matmul(st[0:w, 0:128], T.qs[:, 0:w], kk(j), True, True).then_inc(sem["st%d" % i], 1)
+        g.tensor.matmul(bankS[i][:, 0:w], kk(j), T.qs[:, 0:w], True, False)
+        vwait()
+        g.vector.wait_ge(sem["st%d" % i], 1)
+        a = T.run[0:w, nrun * 64:(nrun + 1) * 64]
+        if i == 0:
+            vop(g.vector.tensor_copy(a, st[0:w, 0:64]))
+        else:
+            vop(g.vector.tensor_tensor(a, st[0:w, 0:64], T.run[0:w, (nrun - 1) * 64:nrun * 64], MAX))
+        vwait()
+        b = T.run[0:w, (nrun + 1) * 64:(nrun + 2) * 64]
+        seen.append(vop(g.vector.tensor_tensor(b, st[0:w, 64:128], a, MAX)))
+        nrun += 2
+
+    cur, lo, width, off = T.run, (nrun - 1) * 64, 64, 0
+    while width > 1:
+        h = width // 2
+        vwait()
+        vop(g.vector.tensor_tensor(T.tr[0:w, off:off + h], cur[0:w, lo:lo + h], cur[0:w, lo + h:lo + 2 * h], MAX))
+        cur, lo, width, off = T.tr, off, h, off + h
+    n_m = vc[0]
+
+    g.tensor.wait_ge(sem.vc, n_m)
+    g.tensor.wait_ge(sem.id2, 16)
+    g.tensor.matmul(T.ps6[0:1, 128:128 + w], T.tr[0:w, lo:lo + 1], T.ident[0:w, 0:w], True, True).then_inc(sem.tm, 1)
+    vwait()
+    g.vector.wait_ge(sem.tm, 1)
+    n_row = vop(g.vector.tensor_copy(T.mrow[0:1, 0:w], T.ps6[0:1, 128:128 + w]))
+    g.tensor.wait_ge(sem.vc, n_row)
+    relu = []
+    for i in range(n):
+        g.tensor.matmul(bankS[i][:, 0:w], T.nh[0:1, 0:128], T.mrow[0:1, 0:w], False, True).then_inc(sem["bm%d" % i], 1)
+        vwait()
+        g.vector.wait_ge(sem["bm%d" % i], 1)
+        relu.append(vop(g.vector.tensor_tensor(T.P[:, i * 128:i * 128 + w], bankS[i][:, 0:w], T.zero[:, 0:w], MAX)))
+
+    g.tensor.wait_ge(sem.ldv, 16)
+    for i, j in enumerate(order):
+        g.tensor.wait_ge(sem.vc, relu[i])
+        ins = g.tensor.matmul(T.ps7[:, 0:w], vv(j), T.P[:, i * 128:i * 128 + w], i == 0, i == n - 1)
+    ins.then_inc(sem.ym, 1)
+    vwait()
+    g.vector.wait_ge(sem.ym, 1)
+    n_y = vop(g.vector.tensor_copy(T.yo[:, 0:w], T.ps7[:, 0:w]))
+    g.sync.wait_ge(sem.vc, n_y)
+    g.sync.dma_start(T.y[:, 0:w], T.yo[:, 0:w]).then_inc(sem.sty, 16)
+    g.sync.wait_ge(sem.sty, 16)
+    g.wait_ge(sem.sent, ne)
+    g.wait_ge(sem.sty, 16)

@@ -2,12 +2,13 @@ from concourse.bass import DstId, RemoteDMATransfer
 from concourse.mybir import dt, AluOpType
 
 NR = 6
+SPLIT = 3
 BF = "bfloat16"
 SCRATCH = {
     "kv": ("sbuf", [128, NR * 256], BF),
     "qs": ("sbuf", [128, 128], BF),
-    "zsrc": ("sbuf", [128, 129], BF),
-    "idd": ("dram", [129, 128], BF),
+    "zsrc": ("sbuf", [128, 128], BF),
+    "idd": ("dram", [128, 128], BF),
     "ident": ("sbuf", [128, 128], BF),
     "zero": ("sbuf", [128, 128], BF),
     "nh": ("sbuf", [128, 128], BF),
@@ -19,8 +20,9 @@ SCRATCH = {
 }
 for _b in range(8):
     SCRATCH["ps%d" % _b] = ("psum", [128, 512], "float32")
-SEMAPHORES = (["ldk", "ldv", "ldq", "id1", "id2", "sent", "vc", "tm", "ym", "sty"]
-              + ["a%d" % j for j in range(NR)] + ["st%d" % j for j in range(NR)] + ["bm%d" % j for j in range(NR)])
+SEMAPHORES = (["ldk", "ldv", "ldq", "pt", "id2", "sent", "vc", "tm", "ym", "sty"]
+              + ["a%d" % j for j in range(NR)] + ["b%d" % j for j in range(NR)] + ["st%d" % j for j in range(NR)]
+              + ["bm%d" % j for j in range(NR)] + ["rl%d" % j for j in range(NR)])
 
 
 def rank_program(g, core, T, topo):
@@ -33,6 +35,7 @@ def rank_program(g, core, T, topo):
     MAX = AluOpType.max
     send_to = [(r + t) % n for t in range(1, n)]
     order = [r] + [(r - t) % n for t in range(1, n)]
+    whole = n - 1 - SPLIT
 
     def slot(j):
         return T.kv[:, j * 256:(j + 1) * 256]
@@ -47,20 +50,6 @@ def rank_program(g, core, T, topo):
     g.scalar.dma_start(vv(r), T.v[:, :]).then_inc(sem.ldv, 16)
     g.sync.dma_start(T.qs[:, 0:w], T.q[:, 0:w]).then_inc(sem.ldq, 16)
 
-    mask = topo.mask(core, T.cores[send_to[0]])
-    for j in send_to:
-        mask &= topo.mask(core, T.cores[j])
-    ne = bin(mask).count("1")
-    ids = []
-    for j in send_to:
-        rid, pid = topo.addr(T.cores[j], core)
-        ids.append(DstId(rid=rid, pnc=pid))
-    g.wait_ge(sem.ldk, 16)
-    g.wait_ge(sem.ldv, 16)
-    g.remote_dma_fused([RemoteDMATransfer(dst_ids=ids, dma_engine_mask=mask, remote_sem=sem["a%d" % r],
-                                          srcs=[slot(r)], dsts=[slot(r) for _ in send_to], alu_op=0)],
-                       local_sem=sem.sent)
-
     vc = [0]
 
     def vop(ins):
@@ -72,18 +61,44 @@ def rank_program(g, core, T, topo):
         if vc[0]:
             g.vector.wait_ge(sem.vc, vc[0])
 
-    vop(g.vector.memset(T.zsrc[:, 1:129], 0.0))
+    vop(g.vector.memset(T.zsrc[:, 1:128], 0.0))
     vwait()
     n_pat = vop(g.vector.memset(T.zsrc[:, 0:1], 1.0))
+    vwait()
+    vop(g.vector.memset(T.ident[:, 127:128], 1.0))
+    vwait()
+    n_col = vop(g.vector.memset(T.ident[0:127, 127:128], 0.0))
     vwait()
     vop(g.vector.memset(T.zero[:, 0:w], 0.0))
     vwait()
     vop(g.vector.memset(T.nh[0:1, :], -0.5))
 
-    g.scalar.wait_ge(sem.vc, n_pat)
-    g.scalar.dma_start(T.idd[:, :], T.zsrc[:, :]).then_inc(sem.id1, 16)
-    g.scalar.wait_ge(sem.id1, 16)
-    g.scalar.dma_start(T.ident[:, :], T.idd[0:128, :]).then_inc(sem.id2, 16)
+    mask = topo.mask(core, T.cores[send_to[0]])
+    for j in send_to:
+        mask &= topo.mask(core, T.cores[j])
+    ne = bin(mask).count("1")
+
+    def send(piece, dests, name):
+        ids = []
+        for j in dests:
+            rid, pid = topo.addr(T.cores[j], core)
+            ids.append(DstId(rid=rid, pnc=pid))
+        g.remote_dma_fused([RemoteDMATransfer(dst_ids=ids, dma_engine_mask=mask, remote_sem=sem[name],
+                                              srcs=[piece], dsts=[piece for _ in dests], alu_op=0)],
+                           local_sem=sem.sent)
+
+    g.wait_ge(sem.vc, n_pat)
+    rid, pid = topo.addr(T.cores[send_to[0]], core)
+    g.remote_dma(T.idd[:, :], T.zsrc[:, :], sem.pt, sem.sent, pid, rid, mask)
+    g.wait_ge(sem.ldk, 16)
+    g.wait_ge(sem.ldv, 16)
+    send(slot(r), send_to[:whole], "a%d" % r)
+    send(kk(r), send_to[whole:], "a%d" % r)
+    send(vv(r), send_to[whole:], "b%d" % r)
+
+    g.scalar.wait_ge(sem.pt, ne)
+    g.scalar.wait_ge(sem.vc, n_col)
+    g.scalar.dma_start(T.ident[:, 0:127], T.idd[0:127, :]).then_inc(sem.id2, 16)
 
     bankS = [T["ps%d" % i] for i in range(n)]
     bankT = [T.ps6, T.ps7]
@@ -121,23 +136,24 @@ def rank_program(g, core, T, topo):
         cur, lo, width, off = T.tr, off, h, off + h
     n_m = vc[0]
 
-    g.tensor.wait_ge(sem.vc, n_m)
     g.tensor.wait_ge(sem.id2, 16)
+    g.tensor.wait_ge(sem.vc, n_m)
     g.tensor.matmul(T.ps6[0:1, 128:128 + w], T.tr[0:w, lo:lo + 1], T.ident[0:w, 0:w], True, True).then_inc(sem.tm, 1)
     vwait()
     g.vector.wait_ge(sem.tm, 1)
     n_row = vop(g.vector.tensor_copy(T.mrow[0:1, 0:w], T.ps6[0:1, 128:128 + w]))
     g.tensor.wait_ge(sem.vc, n_row)
-    relu = []
     for i in range(n):
         g.tensor.matmul(bankS[i][:, 0:w], T.nh[0:1, 0:128], T.mrow[0:1, 0:w], False, True).then_inc(sem["bm%d" % i], 1)
-        vwait()
         g.vector.wait_ge(sem["bm%d" % i], 1)
-        relu.append(vop(g.vector.tensor_tensor(T.P[:, i * 128:i * 128 + w], bankS[i][:, 0:w], T.zero[:, 0:w], MAX)))
+        g.vector.tensor_tensor(T.P[:, i * 128:i * 128 + w], bankS[i][:, 0:w], T.zero[:, 0:w],
+                               MAX).then_inc(sem["rl%d" % i], 1)
 
     g.tensor.wait_ge(sem.ldv, 16)
     for i, j in enumerate(order):
-        g.tensor.wait_ge(sem.vc, relu[i])
+        g.tensor.wait_ge(sem["rl%d" % i], 1)
+        if i > whole:
+            g.tensor.wait_ge(sem["b%d" % j], ne)
         ins = g.tensor.matmul(T.ps7[:, 0:w], vv(j), T.P[:, i * 128:i * 128 + w], i == 0, i == n - 1)
     ins.then_inc(sem.ym, 1)
     vwait()
@@ -146,5 +162,5 @@ def rank_program(g, core, T, topo):
     g.sync.wait_ge(sem.vc, n_y)
     g.sync.dma_start(T.y[:, 0:w], T.yo[:, 0:w]).then_inc(sem.sty, 16)
     g.sync.wait_ge(sem.sty, 16)
-    g.wait_ge(sem.sent, ne)
+    g.wait_ge(sem.sent, 4 * ne)
     g.wait_ge(sem.sty, 16)

@@ -5,6 +5,7 @@ NR = 6
 SPLIT = 3
 BF = "bfloat16"
 SCRATCH = {
+    "kd": ("dram", [128, 128], BF),
     "kv": ("sbuf", [128, NR * 256], BF),
     "qs": ("sbuf", [128, 128], BF),
     "zsrc": ("sbuf", [128, 128], BF),
@@ -20,7 +21,7 @@ SCRATCH = {
 }
 for _b in range(8):
     SCRATCH["ps%d" % _b] = ("psum", [128, 512], "float32")
-SEMAPHORES = (["ldk", "ldv", "ldq", "pt", "id2", "sent", "vc", "tm", "ym", "sty"]
+SEMAPHORES = (["ldd", "ldk", "ldv", "ldq", "pm", "pt", "id2", "sent", "vc", "tm", "ym", "sty"]
               + ["a%d" % j for j in range(NR)] + ["b%d" % j for j in range(NR)] + ["st%d" % j for j in range(NR)]
               + ["bm%d" % j for j in range(NR)] + ["rl%d" % j for j in range(NR)])
 
@@ -35,7 +36,8 @@ def rank_program(g, core, T, topo):
     MAX = AluOpType.max
     send_to = [(r + t) % n for t in range(1, n)]
     order = [r] + [(r - t) % n for t in range(1, n)]
-    whole = n - 1 - SPLIT
+    late = list(range(1, SPLIT + 1))
+    finish = [0] + list(range(SPLIT + 1, n)) + late
 
     def slot(j):
         return T.kv[:, j * 256:(j + 1) * 256]
@@ -46,10 +48,13 @@ def rank_program(g, core, T, topo):
     def vv(j):
         return T.kv[:, j * 256 + 128:(j + 1) * 256]
 
-    g.sync.dma_start(kk(r), T.k[:, :]).then_inc(sem.ldk, 16)
+    g.sync.dma_start(T.kd[:, :], T.k[:, :]).then_inc(sem.ldd, 16)
     g.scalar.dma_start(vv(r), T.v[:, :]).then_inc(sem.ldv, 16)
+    g.sync.dma_start(kk(r), T.k[:, :]).then_inc(sem.ldk, 16)
     g.sync.dma_start(T.qs[:, 0:w], T.q[:, 0:w]).then_inc(sem.ldq, 16)
 
+    g.vector.memset(T.zsrc[:, 0:1], 1.0).then_inc(sem.pm, 1)
+    g.vector.memset(T.zsrc[:, 1:128], 0.0).then_inc(sem.pm, 1)
     vc = [0]
 
     def vop(ins):
@@ -61,10 +66,6 @@ def rank_program(g, core, T, topo):
         if vc[0]:
             g.vector.wait_ge(sem.vc, vc[0])
 
-    vop(g.vector.memset(T.zsrc[:, 1:128], 0.0))
-    vwait()
-    n_pat = vop(g.vector.memset(T.zsrc[:, 0:1], 1.0))
-    vwait()
     vop(g.vector.memset(T.ident[:, 127:128], 1.0))
     vwait()
     n_col = vop(g.vector.memset(T.ident[0:127, 127:128], 0.0))
@@ -78,23 +79,24 @@ def rank_program(g, core, T, topo):
         mask &= topo.mask(core, T.cores[j])
     ne = bin(mask).count("1")
 
-    def send(piece, dests, name):
+    def send(src, piece, dests, name):
         ids = []
         for j in dests:
             rid, pid = topo.addr(T.cores[j], core)
             ids.append(DstId(rid=rid, pnc=pid))
         g.remote_dma_fused([RemoteDMATransfer(dst_ids=ids, dma_engine_mask=mask, remote_sem=sem[name],
-                                              srcs=[piece], dsts=[piece for _ in dests], alu_op=0)],
+                                              srcs=[src], dsts=[piece for _ in dests], alu_op=0)],
                            local_sem=sem.sent)
 
-    g.wait_ge(sem.vc, n_pat)
+    g.wait_ge(sem.pm, 2)
     rid, pid = topo.addr(T.cores[send_to[0]], core)
     g.remote_dma(T.idd[:, :], T.zsrc[:, :], sem.pt, sem.sent, pid, rid, mask)
+    g.wait_ge(sem.ldd, 16)
+    send(T.kd[:, :], kk(r), send_to[:SPLIT], "a%d" % r)
     g.wait_ge(sem.ldk, 16)
     g.wait_ge(sem.ldv, 16)
-    send(slot(r), send_to[:whole], "a%d" % r)
-    send(kk(r), send_to[whole:], "a%d" % r)
-    send(vv(r), send_to[whole:], "b%d" % r)
+    send(slot(r), slot(r), send_to[SPLIT:], "a%d" % r)
+    send(vv(r), vv(r), send_to[:SPLIT], "b%d" % r)
 
     g.scalar.wait_ge(sem.pt, ne)
     g.scalar.wait_ge(sem.vc, n_col)
@@ -143,18 +145,19 @@ def rank_program(g, core, T, topo):
     g.vector.wait_ge(sem.tm, 1)
     n_row = vop(g.vector.tensor_copy(T.mrow[0:1, 0:w], T.ps6[0:1, 128:128 + w]))
     g.tensor.wait_ge(sem.vc, n_row)
-    for i in range(n):
+    for i in finish:
         g.tensor.matmul(bankS[i][:, 0:w], T.nh[0:1, 0:128], T.mrow[0:1, 0:w], False, True).then_inc(sem["bm%d" % i], 1)
         g.vector.wait_ge(sem["bm%d" % i], 1)
         g.vector.tensor_tensor(T.P[:, i * 128:i * 128 + w], bankS[i][:, 0:w], T.zero[:, 0:w],
                                MAX).then_inc(sem["rl%d" % i], 1)
 
     g.tensor.wait_ge(sem.ldv, 16)
-    for i, j in enumerate(order):
+    for c, i in enumerate(finish):
+        j = order[i]
         g.tensor.wait_ge(sem["rl%d" % i], 1)
-        if i > whole:
+        if i in late:
             g.tensor.wait_ge(sem["b%d" % j], ne)
-        ins = g.tensor.matmul(T.ps7[:, 0:w], vv(j), T.P[:, i * 128:i * 128 + w], i == 0, i == n - 1)
+        ins = g.tensor.matmul(T.ps7[:, 0:w], vv(j), T.P[:, i * 128:i * 128 + w], c == 0, c == n - 1)
     ins.then_inc(sem.ym, 1)
     vwait()
     g.vector.wait_ge(sem.ym, 1)

@@ -1,46 +1,77 @@
 from concourse.bass import DstId, RemoteDMATransfer
-from concourse.mybir import dt, AluOpType
+from concourse.mybir import dt, AluOpType, AxisListType
 
 NR = 6
-SPLIT = 3
 BF = "bfloat16"
+K_BY = {1: "R", 2: "R", 3: "R", 4: "A", 5: "A"}
+V_BY = {1: "B", 2: "B", 3: "B", 4: "R", 5: "A"}
+K_SEQ = [0, 1, 2, 4, 3, 5]
+V_SEQ = [0, 1, 4, 2, 5, 3]
 SCRATCH = {
     "kd": ("dram", [128, 128], BF),
+    "vd": ("dram", [128, 128], BF),
     "kv": ("sbuf", [128, NR * 256], BF),
     "qs": ("sbuf", [128, 128], BF),
     "zsrc": ("sbuf", [128, 128], BF),
     "idd": ("dram", [128, 128], BF),
     "ident": ("sbuf", [128, 128], BF),
+    "cst": ("sbuf", [128, 128], BF),
     "zero": ("sbuf", [128, 128], BF),
     "nh": ("sbuf", [128, 128], BF),
-    "mrow": ("sbuf", [128, 128], BF),
-    "run": ("sbuf", [128, 2 * NR * 64], BF),
-    "tr": ("sbuf", [128, 64], BF),
+    "mc": ("sbuf", [128, 8], "float32"),
+    "mm": ("sbuf", [128, 8], "float32"),
+    "diag": ("sbuf", [128, 128], BF),
     "P": ("sbuf", [128, NR * 128], BF),
     "yo": ("sbuf", [128, 128], BF),
 }
 for _b in range(8):
     SCRATCH["ps%d" % _b] = ("psum", [128, 512], "float32")
-SEMAPHORES = (["ldd", "ldk", "ldv", "ldq", "pm", "pt", "id2", "sent", "vc", "tm", "ym", "sty"]
+SEMAPHORES = (["ldd", "lde", "ldk", "ldv", "ldq", "pm", "pt", "id2", "sent", "vc", "ym", "sty", "hk", "hv", "cn", "cz"]
               + ["a%d" % j for j in range(NR)] + ["b%d" % j for j in range(NR)] + ["st%d" % j for j in range(NR)]
               + ["bm%d" % j for j in range(NR)] + ["rl%d" % j for j in range(NR)])
 
 
+def _bits(m):
+    return bin(m).count("1")
+
+
+def _same_chip(topo, a, b):
+    return topo.host(a) == topo.host(b) and topo.chip(a) == topo.chip(b)
+
+
+def _team(T, topo, R):
+    total = topo.CORES_PER_HOST * (1 + max(topo.host(c) for c in T.cores))
+    far = [c for c in range(total)
+           if _same_chip(topo, c, R) and c not in T.cores and topo.die(c) != topo.die(R)
+           and all(topo.may_write(c, d) for d in T.cores if d != R)]
+    return {"R": R, "A": far[0], "B": far[1]}
+
+
+def _off_mask(T, topo, c):
+    m = -1
+    for d in T.cores:
+        if not _same_chip(topo, c, d):
+            m &= topo.mask(c, d)
+    return m
+
+
 def rank_program(g, core, T, topo):
-    r = T.rank_of(core)
-    if r is None:
-        return
     n = len(T.cores)
-    w = T.tables["WID"][r]
     sem = T.sem
     MAX = AluOpType.max
-    send_to = [(r + t) % n for t in range(1, n)]
-    order = [r] + [(r - t) % n for t in range(1, n)]
-    late = list(range(1, SPLIT + 1))
-    finish = [0] + list(range(SPLIT + 1, n)) + late
-
-    def slot(j):
-        return T.kv[:, j * 256:(j + 1) * 256]
+    teams = [_team(T, topo, R) for R in T.cores]
+    mine = [(r, role) for r, tm in enumerate(teams) for role in tm if tm[role] == core]
+    if not mine:
+        return
+    r, role = mine[0]
+    tm = teams[r]
+    mask = _off_mask(T, topo, core)
+    ne = _bits(mask)
+    R = tm["R"]
+    on_mask = topo.mask(R, tm["A"]) & topo.mask(R, tm["B"]) & ~_off_mask(T, topo, R)
+    if not on_mask:
+        on_mask = _off_mask(T, topo, R)
+    non = _bits(on_mask)
 
     def kk(j):
         return T.kv[:, j * 256:j * 256 + 128]
@@ -48,10 +79,44 @@ def rank_program(g, core, T, topo):
     def vv(j):
         return T.kv[:, j * 256 + 128:(j + 1) * 256]
 
+    def send(src, piece, dest_cores, name, msk):
+        ids = []
+        for d in dest_cores:
+            rid, pid = topo.addr(d, core)
+            ids.append(DstId(rid=rid, pnc=pid))
+        g.remote_dma_fused([RemoteDMATransfer(dst_ids=ids, dma_engine_mask=msk, remote_sem=sem[name],
+                                              srcs=[src], dsts=[piece for _ in dest_cores], alu_op=0)],
+                           local_sem=sem.sent)
+
+    def served(table):
+        return [T.cores[(r + t) % n] for t in range(1, n) if table[t] == role]
+
+    if role != "R":
+        g.vector.memset(T.cst[:, :], -0.5 if role == "A" else 0.0).then_inc(sem.pm, 1)
+        g.wait_ge(sem.pm, 1)
+        rid, pid = topo.addr(R, core)
+        if role == "A":
+            g.remote_dma(T.nh[:, :], T.cst[:, :], sem.cn, sem.sent, pid, rid, mask & topo.mask(core, R))
+        else:
+            g.remote_dma(T.zero[:, :], T.cst[:, :], sem.cz, sem.sent, pid, rid, mask & topo.mask(core, R))
+        calls = 1
+        if served(K_BY):
+            g.wait_ge(sem.hk, non)
+            send(T.kd[:, :], kk(r), served(K_BY), "a%d" % r, mask)
+            calls += 1
+        g.wait_ge(sem.hv, non)
+        send(T.vd[:, :], vv(r), served(V_BY), "b%d" % r, mask)
+        calls += 1
+        g.wait_ge(sem.sent, calls * ne)
+        return
+
+    w = T.tables["WID"][r]
+
     g.sync.dma_start(T.kd[:, :], T.k[:, :]).then_inc(sem.ldd, 16)
-    g.scalar.dma_start(vv(r), T.v[:, :]).then_inc(sem.ldv, 16)
+    g.scalar.dma_start(T.vd[:, :], T.v[:, :]).then_inc(sem.lde, 16)
     g.sync.dma_start(kk(r), T.k[:, :]).then_inc(sem.ldk, 16)
-    g.sync.dma_start(T.qs[:, 0:w], T.q[:, 0:w]).then_inc(sem.ldq, 16)
+    g.scalar.dma_start(T.qs[:, 0:w], T.q[:, 0:w]).then_inc(sem.ldq, 16)
+    g.sync.dma_start(vv(r), T.v[:, :]).then_inc(sem.ldv, 16)
 
     g.vector.memset(T.zsrc[:, 0:1], 1.0).then_inc(sem.pm, 1)
     g.vector.memset(T.zsrc[:, 1:128], 0.0).then_inc(sem.pm, 1)
@@ -69,95 +134,67 @@ def rank_program(g, core, T, topo):
     vop(g.vector.memset(T.ident[:, 127:128], 1.0))
     vwait()
     n_col = vop(g.vector.memset(T.ident[0:127, 127:128], 0.0))
-    vwait()
-    vop(g.vector.memset(T.zero[:, 0:w], 0.0))
-    vwait()
-    vop(g.vector.memset(T.nh[0:1, :], -0.5))
-
-    mask = topo.mask(core, T.cores[send_to[0]])
-    for j in send_to:
-        mask &= topo.mask(core, T.cores[j])
-    ne = bin(mask).count("1")
-
-    def send(src, piece, dests, name):
-        ids = []
-        for j in dests:
-            rid, pid = topo.addr(T.cores[j], core)
-            ids.append(DstId(rid=rid, pnc=pid))
-        g.remote_dma_fused([RemoteDMATransfer(dst_ids=ids, dma_engine_mask=mask, remote_sem=sem[name],
-                                              srcs=[src], dsts=[piece for _ in dests], alu_op=0)],
-                           local_sem=sem.sent)
 
     g.wait_ge(sem.pm, 2)
-    rid, pid = topo.addr(T.cores[send_to[0]], core)
+    rid, pid = topo.addr(T.cores[(r + 1) % n], core)
     g.remote_dma(T.idd[:, :], T.zsrc[:, :], sem.pt, sem.sent, pid, rid, mask)
     g.wait_ge(sem.ldd, 16)
-    send(T.kd[:, :], kk(r), send_to[:SPLIT], "a%d" % r)
-    g.wait_ge(sem.ldk, 16)
-    g.wait_ge(sem.ldv, 16)
-    send(slot(r), slot(r), send_to[SPLIT:], "a%d" % r)
-    send(vv(r), vv(r), send_to[:SPLIT], "b%d" % r)
+    send(T.kd[:, :], T.kd[:, :], [tm["A"]], "hk", on_mask)
+    send(T.kd[:, :], kk(r), served(K_BY), "a%d" % r, mask)
+    g.wait_ge(sem.lde, 16)
+    send(T.vd[:, :], T.vd[:, :], [tm["B"], tm["A"]], "hv", on_mask)
+    send(T.vd[:, :], vv(r), served(V_BY), "b%d" % r, mask)
+    n_sent = 3 * ne + 2 * non
 
     g.scalar.wait_ge(sem.pt, ne)
     g.scalar.wait_ge(sem.vc, n_col)
     g.scalar.dma_start(T.ident[:, 0:127], T.idd[0:127, :]).then_inc(sem.id2, 16)
+
+    def arrival(table, t):
+        return _bits(_off_mask(T, topo, teams[(r - t) % n][table[t]]))
 
     bankS = [T["ps%d" % i] for i in range(n)]
     bankT = [T.ps6, T.ps7]
 
     g.tensor.wait_ge(sem.ldq, 16)
     seen = []
-    nrun = 0
-    for i, j in enumerate(order):
-        if i == 0:
+    for p, t in enumerate(K_SEQ):
+        j = (r - t) % n
+        if t == 0:
             g.tensor.wait_ge(sem.ldk, 16)
         else:
-            g.tensor.wait_ge(sem["a%d" % j], ne)
-        if i >= 2:
-            g.tensor.wait_ge(sem.vc, seen[i - 2])
-        st = bankT[i % 2]
-        g.tensor.matmul(st[0:w, 0:128], T.qs[:, 0:w], kk(j), True, True).then_inc(sem["st%d" % i], 1)
-        g.tensor.matmul(bankS[i][:, 0:w], kk(j), T.qs[:, 0:w], True, False)
+            g.tensor.wait_ge(sem["a%d" % j], arrival(K_BY, t))
+        if p >= 2:
+            g.tensor.wait_ge(sem.vc, seen[p - 2])
+        st = bankT[p % 2]
+        g.tensor.matmul(st[0:w, 0:128], T.qs[:, 0:w], kk(j), True, True).then_inc(sem["st%d" % p], 1)
+        g.tensor.matmul(bankS[t][:, 0:w], kk(j), T.qs[:, 0:w], True, False)
         vwait()
-        g.vector.wait_ge(sem["st%d" % i], 1)
-        a = T.run[0:w, nrun * 64:(nrun + 1) * 64]
-        if i == 0:
-            vop(g.vector.tensor_copy(a, st[0:w, 0:64]))
-        else:
-            vop(g.vector.tensor_tensor(a, st[0:w, 0:64], T.run[0:w, (nrun - 1) * 64:nrun * 64], MAX))
-        vwait()
-        b = T.run[0:w, (nrun + 1) * 64:(nrun + 2) * 64]
-        seen.append(vop(g.vector.tensor_tensor(b, st[0:w, 64:128], a, MAX)))
-        nrun += 2
+        g.vector.wait_ge(sem["st%d" % p], 1)
+        seen.append(vop(g.vector.tensor_reduce(T.mc[0:w, p:p + 1], st[0:w, 0:128], AxisListType.X, MAX)))
 
-    cur, lo, width, off = T.run, (nrun - 1) * 64, 64, 0
-    while width > 1:
-        h = width // 2
-        vwait()
-        vop(g.vector.tensor_tensor(T.tr[0:w, off:off + h], cur[0:w, lo:lo + h], cur[0:w, lo + h:lo + 2 * h], MAX))
-        cur, lo, width, off = T.tr, off, h, off + h
-    n_m = vc[0]
-
-    g.tensor.wait_ge(sem.id2, 16)
-    g.tensor.wait_ge(sem.vc, n_m)
-    g.tensor.matmul(T.ps6[0:1, 128:128 + w], T.tr[0:w, lo:lo + 1], T.ident[0:w, 0:w], True, True).then_inc(sem.tm, 1)
     vwait()
-    g.vector.wait_ge(sem.tm, 1)
-    n_row = vop(g.vector.tensor_copy(T.mrow[0:1, 0:w], T.ps6[0:1, 128:128 + w]))
-    g.tensor.wait_ge(sem.vc, n_row)
-    for i in finish:
-        g.tensor.matmul(bankS[i][:, 0:w], T.nh[0:1, 0:128], T.mrow[0:1, 0:w], False, True).then_inc(sem["bm%d" % i], 1)
-        g.vector.wait_ge(sem["bm%d" % i], 1)
-        g.vector.tensor_tensor(T.P[:, i * 128:i * 128 + w], bankS[i][:, 0:w], T.zero[:, 0:w],
-                               MAX).then_inc(sem["rl%d" % i], 1)
+    vop(g.vector.tensor_reduce(T.mm[0:w, 0:1], T.mc[0:w, 0:n], AxisListType.X, MAX))
+    vwait()
+    g.vector.wait_ge(sem.id2, 16)
+    n_diag = vop(g.vector.tensor_scalar(T.diag[0:w, 0:w], T.ident[0:w, 0:w], T.mm[0:w, 0:1], None, AluOpType.mult))
+    g.tensor.wait_ge(sem.cn, _bits(_off_mask(T, topo, tm["A"])))
+    g.tensor.wait_ge(sem.vc, n_diag)
+    g.vector.wait_ge(sem.cz, _bits(_off_mask(T, topo, tm["B"])))
+    for t in V_SEQ:
+        g.tensor.matmul(bankS[t][:, 0:w], T.nh[0:w, 0:128], T.diag[0:w, 0:w], False, True).then_inc(sem["bm%d" % t], 1)
+        g.vector.wait_ge(sem["bm%d" % t], 1)
+        g.vector.tensor_tensor(T.P[:, t * 128:t * 128 + w], bankS[t][:, 0:w], T.zero[:, 0:w],
+                               MAX).then_inc(sem["rl%d" % t], 1)
 
-    g.tensor.wait_ge(sem.ldv, 16)
-    for c, i in enumerate(finish):
-        j = order[i]
-        g.tensor.wait_ge(sem["rl%d" % i], 1)
-        if i in late:
-            g.tensor.wait_ge(sem["b%d" % j], ne)
-        ins = g.tensor.matmul(T.ps7[:, 0:w], vv(j), T.P[:, i * 128:i * 128 + w], c == 0, c == n - 1)
+    for c, t in enumerate(V_SEQ):
+        j = (r - t) % n
+        g.tensor.wait_ge(sem["rl%d" % t], 1)
+        if t == 0:
+            g.tensor.wait_ge(sem.ldv, 16)
+        else:
+            g.tensor.wait_ge(sem["b%d" % j], arrival(V_BY, t))
+        ins = g.tensor.matmul(T.ps7[:, 0:w], vv(j), T.P[:, t * 128:t * 128 + w], c == 0, c == n - 1)
     ins.then_inc(sem.ym, 1)
     vwait()
     g.vector.wait_ge(sem.ym, 1)
@@ -165,5 +202,5 @@ def rank_program(g, core, T, topo):
     g.sync.wait_ge(sem.vc, n_y)
     g.sync.dma_start(T.y[:, 0:w], T.yo[:, 0:w]).then_inc(sem.sty, 16)
     g.sync.wait_ge(sem.sty, 16)
-    g.wait_ge(sem.sent, 4 * ne)
+    g.wait_ge(sem.sent, n_sent)
     g.wait_ge(sem.sty, 16)

from concourse.bass import DstId, RemoteDMATransfer
from concourse.mybir import dt, AluOpType, AxisListType

NR = 6
BF = "bfloat16"
K_BY = {1: "R", 2: "R", 3: "R", 4: "A", 5: "A"}
V_BY = {1: "B", 2: "B", 3: "B", 4: "R", 5: "A"}
K_SEQ = [0, 1, 2, 4, 3, 5]
V_SEQ = [0, 1, 4, 2, 5, 3]
SCRATCH = {
    "kd": ("dram", [128, 128], BF),
    "vd": ("dram", [128, 128], BF),
    "kv": ("sbuf", [128, NR * 256], BF),
    "qs": ("sbuf", [128, 128], BF),
    "zsrc": ("sbuf", [128, 128], BF),
    "idd": ("dram", [128, 128], BF),
    "ident": ("sbuf", [128, 128], BF),
    "cst": ("sbuf", [128, 128], BF),
    "zero": ("sbuf", [128, 128], BF),
    "nh": ("sbuf", [128, 128], BF),
    "mc": ("sbuf", [128, 8], "float32"),
    "mm": ("sbuf", [128, 8], "float32"),
    "diag": ("sbuf", [128, 128], BF),
    "P": ("sbuf", [128, NR * 128], BF),
    "yo": ("sbuf", [128, 128], BF),
}
for _b in range(8):
    SCRATCH["ps%d" % _b] = ("psum", [128, 512], "float32")
SEMAPHORES = (["ldd", "lde", "ldk", "ldv", "ldq", "pm", "pt", "id2", "sent", "vc", "ym", "sty", "hk", "hv", "cn", "cz"]
              + ["a%d" % j for j in range(NR)] + ["b%d" % j for j in range(NR)] + ["st%d" % j for j in range(NR)]
              + ["bm%d" % j for j in range(NR)] + ["rl%d" % j for j in range(NR)])


def _bits(m):
    return bin(m).count("1")


def _same_chip(topo, a, b):
    return topo.host(a) == topo.host(b) and topo.chip(a) == topo.chip(b)


def _team(T, topo, R):
    total = topo.CORES_PER_HOST * (1 + max(topo.host(c) for c in T.cores))
    far = [c for c in range(total)
           if _same_chip(topo, c, R) and c not in T.cores and topo.die(c) != topo.die(R)
           and all(topo.may_write(c, d) for d in T.cores if d != R)]
    return {"R": R, "A": far[0], "B": far[1]}


def _off_mask(T, topo, c):
    m = -1
    for d in T.cores:
        if not _same_chip(topo, c, d):
            m &= topo.mask(c, d)
    return m


def rank_program(g, core, T, topo):
    n = len(T.cores)
    sem = T.sem
    MAX = AluOpType.max
    teams = [_team(T, topo, R) for R in T.cores]
    mine = [(r, role) for r, tm in enumerate(teams) for role in tm if tm[role] == core]
    if not mine:
        return
    r, role = mine[0]
    tm = teams[r]
    mask = _off_mask(T, topo, core)
    ne = _bits(mask)
    R = tm["R"]
    on_mask = topo.mask(R, tm["A"]) & topo.mask(R, tm["B"]) & ~_off_mask(T, topo, R)
    if not on_mask:
        on_mask = _off_mask(T, topo, R)
    non = _bits(on_mask)

    def kk(j):
        return T.kv[:, j * 256:j * 256 + 128]

    def vv(j):
        return T.kv[:, j * 256 + 128:(j + 1) * 256]

    def send(src, piece, dest_cores, name, msk):
        ids = []
        for d in dest_cores:
            rid, pid = topo.addr(d, core)
            ids.append(DstId(rid=rid, pnc=pid))
        g.remote_dma_fused([RemoteDMATransfer(dst_ids=ids, dma_engine_mask=msk, remote_sem=sem[name],
                                              srcs=[src], dsts=[piece for _ in dest_cores], alu_op=0)],
                           local_sem=sem.sent)

    def served(table):
        return [T.cores[(r + t) % n] for t in range(1, n) if table[t] == role]

    if role != "R":
        g.vector.memset(T.cst[:, :], -0.5 if role == "A" else 0.0).then_inc(sem.pm, 1)
        g.wait_ge(sem.pm, 1)
        rid, pid = topo.addr(R, core)
        if role == "A":
            g.remote_dma(T.nh[:, :], T.cst[:, :], sem.cn, sem.sent, pid, rid, mask & topo.mask(core, R))
        else:
            g.remote_dma(T.zero[:, :], T.cst[:, :], sem.cz, sem.sent, pid, rid, mask & topo.mask(core, R))
        calls = 1
        if served(K_BY):
            g.wait_ge(sem.hk, non)
            send(T.kd[:, :], kk(r), served(K_BY), "a%d" % r, mask)
            calls += 1
        g.wait_ge(sem.hv, non)
        send(T.vd[:, :], vv(r), served(V_BY), "b%d" % r, mask)
        calls += 1
        g.wait_ge(sem.sent, calls * ne)
        return

    w = T.tables["WID"][r]

    g.sync.dma_start(T.kd[:, :], T.k[:, :]).then_inc(sem.ldd, 16)
    g.scalar.dma_start(T.vd[:, :], T.v[:, :]).then_inc(sem.lde, 16)
    g.sync.dma_start(kk(r), T.k[:, :]).then_inc(sem.ldk, 16)
    g.scalar.dma_start(T.qs[:, 0:w], T.q[:, 0:w]).then_inc(sem.ldq, 16)
    g.sync.dma_start(vv(r), T.v[:, :]).then_inc(sem.ldv, 16)

    g.vector.memset(T.zsrc[:, 0:1], 1.0).then_inc(sem.pm, 1)
    g.vector.memset(T.zsrc[:, 1:128], 0.0).then_inc(sem.pm, 1)
    vc = [0]

    def vop(ins):
        ins.then_inc(sem.vc, 1)
        vc[0] += 1
        return vc[0]

    def vwait():
        if vc[0]:
            g.vector.wait_ge(sem.vc, vc[0])

    vop(g.vector.memset(T.ident[:, 127:128], 1.0))
    vwait()
    n_col = vop(g.vector.memset(T.ident[0:127, 127:128], 0.0))

    g.wait_ge(sem.pm, 2)
    rid, pid = topo.addr(T.cores[(r + 1) % n], core)
    g.remote_dma(T.idd[:, :], T.zsrc[:, :], sem.pt, sem.sent, pid, rid, mask)
    g.wait_ge(sem.ldd, 16)
    send(T.kd[:, :], T.kd[:, :], [tm["A"]], "hk", on_mask)
    send(T.kd[:, :], kk(r), served(K_BY), "a%d" % r, mask)
    g.wait_ge(sem.lde, 16)
    send(T.vd[:, :], T.vd[:, :], [tm["B"], tm["A"]], "hv", on_mask)
    send(T.vd[:, :], vv(r), served(V_BY), "b%d" % r, mask)
    n_sent = 3 * ne + 2 * non

    g.scalar.wait_ge(sem.pt, ne)
    g.scalar.wait_ge(sem.vc, n_col)
    g.scalar.dma_start(T.ident[:, 0:127], T.idd[0:127, :]).then_inc(sem.id2, 16)

    def arrival(table, t):
        return _bits(_off_mask(T, topo, teams[(r - t) % n][table[t]]))

    bankS = [T["ps%d" % i] for i in range(n)]
    bankT = [T.ps6, T.ps7]

    g.tensor.wait_ge(sem.ldq, 16)
    seen = []
    for p, t in enumerate(K_SEQ):
        j = (r - t) % n
        if t == 0:
            g.tensor.wait_ge(sem.ldk, 16)
        else:
            g.tensor.wait_ge(sem["a%d" % j], arrival(K_BY, t))
        if p >= 2:
            g.tensor.wait_ge(sem.vc, seen[p - 2])
        st = bankT[p % 2]
        g.tensor.matmul(st[0:w, 0:128], T.qs[:, 0:w], kk(j), True, True).then_inc(sem["st%d" % p], 1)
        g.tensor.matmul(bankS[t][:, 0:w], kk(j), T.qs[:, 0:w], True, False)
        vwait()
        g.vector.wait_ge(sem["st%d" % p], 1)
        seen.append(vop(g.vector.tensor_reduce(T.mc[0:w, p:p + 1], st[0:w, 0:128], AxisListType.X, MAX)))

    vwait()
    vop(g.vector.tensor_reduce(T.mm[0:w, 0:1], T.mc[0:w, 0:n], AxisListType.X, MAX))
    vwait()
    g.vector.wait_ge(sem.id2, 16)
    n_diag = vop(g.vector.tensor_scalar(T.diag[0:w, 0:w], T.ident[0:w, 0:w], T.mm[0:w, 0:1], None, AluOpType.mult))
    g.tensor.wait_ge(sem.cn, _bits(_off_mask(T, topo, tm["A"])))
    g.tensor.wait_ge(sem.vc, n_diag)
    g.vector.wait_ge(sem.cz, _bits(_off_mask(T, topo, tm["B"])))
    for t in V_SEQ:
        g.tensor.matmul(bankS[t][:, 0:w], T.nh[0:w, 0:128], T.diag[0:w, 0:w], False, True).then_inc(sem["bm%d" % t], 1)
        g.vector.wait_ge(sem["bm%d" % t], 1)
        g.vector.tensor_tensor(T.P[:, t * 128:t * 128 + w], bankS[t][:, 0:w], T.zero[:, 0:w],
                               MAX).then_inc(sem["rl%d" % t], 1)

    for c, t in enumerate(V_SEQ):
        j = (r - t) % n
        g.tensor.wait_ge(sem["rl%d" % t], 1)
        if t == 0:
            g.tensor.wait_ge(sem.ldv, 16)
        else:
            g.tensor.wait_ge(sem["b%d" % j], arrival(V_BY, t))
        ins = g.tensor.matmul(T.ps7[:, 0:w], vv(j), T.P[:, t * 128:t * 128 + w], c == 0, c == n - 1)
    ins.then_inc(sem.ym, 1)
    vwait()
    g.vector.wait_ge(sem.ym, 1)
    n_y = vop(g.vector.tensor_copy(T.yo[:, 0:w], T.ps7[:, 0:w]))
    g.sync.wait_ge(sem.vc, n_y)
    g.sync.dma_start(T.y[:, 0:w], T.yo[:, 0:w]).then_inc(sem.sty, 16)
    g.sync.wait_ge(sem.sty, 16)
    g.wait_ge(sem.sent, n_sent)
    g.wait_ge(sem.sty, 16)
